import numpy as np
import ml_dtypes


def mxq(x, axis, fmt="e4m3"):
    dtype, down = {"e4m3": (ml_dtypes.float8_e4m3fn, 7), "e5m2": (ml_dtypes.float8_e5m2, 14)}[fmt]
    v = np.moveaxis(np.asarray(x, np.float32).astype(ml_dtypes.bfloat16).astype(np.float64), axis, -1)
    blocks = v.reshape(v.shape[:-1] + (-1, 32))
    amax = np.abs(blocks).max(-1, keepdims=True)
    byte = np.maximum(np.where(amax > 0, np.frexp(amax)[1] - 1 + 127, 0) - down, 1)
    scale = np.exp2(byte - 127.0)
    codes = (blocks / scale).astype(np.float32).astype(dtype).astype(np.float64)
    return np.moveaxis((codes * scale).reshape(v.shape), -1, axis)


WIDE = False


def mx_kscale(k):
    if not WIDE:
        return np.ones(k)
    levels = np.array([10, -10, 5, -5, 0])
    if k % 512:
        return np.exp2(np.random.permutation(np.resize(levels, k // 32))).repeat(32)
    a = np.empty((k // 512, 16))
    for p in range(k // 512):
        a[p, :8] = np.random.permutation(np.resize(levels, 8))
        for g in range(8):
            far = levels[np.abs(levels - a[p, g]) >= 10]
            a[p, g + 8] = far[np.random.randint(len(far))]
    return np.exp2(a.ravel()).repeat(32)


BF16 = ml_dtypes.bfloat16


def bf(x):
    return np.asarray(x, np.float32).astype(BF16)


def f64(x):
    return np.asarray(x).astype(np.float64)


E2M1 = np.array([0.0, 0.5, 1.0, 1.5, 2.0, 3.0, 4.0, 6.0, -0.0, -0.5, -1.0, -1.5, -2.0, -3.0, -4.0, -6.0])


def pack_weight(w, fmt):
    k, n = w.shape
    w = f64(bf(w)).reshape(k // 32, 32, n)
    amax = np.abs(w).max(1)
    if fmt == "e4m3":
        byte = np.frexp(amax)[1] - 1 + 127 - 7
    else:
        mant, ex = np.frexp(amax / 6.0)
        byte = np.where(mant > 0.5, ex, ex - 1) + 127
    byte = np.clip(np.where(amax > 0, byte, 1), 1, 254)
    scaled = (w * np.exp2(127.0 - byte)[:, None, :]).reshape(k, n).astype(np.float32)
    by_word = np.ascontiguousarray(scaled.reshape(k // 512, 128, 4, n).transpose(0, 1, 3, 2))
    if fmt == "e4m3":
        words = by_word.astype(ml_dtypes.float8_e4m3fn).view(np.uint8)
    else:
        c = by_word.astype(ml_dtypes.float4_e2m1fn).view(np.uint8) & 0xF
        words = c[..., 0::2] | (c[..., 1::2] << 4)
    return np.ascontiguousarray(words), np.ascontiguousarray(byte.astype(np.uint8).reshape(k // 512, 16, n))


def unpack_weight(words, scales, fmt):
    g, p, n, _ = words.shape
    if fmt == "e4m3":
        vals = np.ascontiguousarray(words).view(ml_dtypes.float8_e4m3fn).astype(np.float64)
    else:
        nib = np.empty((g, p, n, 4), np.uint8)
        nib[..., 0::2] = words & 0xF
        nib[..., 1::2] = words >> 4
        vals = E2M1[nib]
    vals = vals * np.repeat(np.exp2(scales.astype(np.float64) - 127.0), 8, axis=1)[..., None]
    return vals.transpose(0, 1, 3, 2).reshape(g * 512, n)
def pack4(w):
    words, scales = pack_weight(w, "e2m1")
    return words.reshape(words.shape[0], 128, -1), scales


def unpack4(words, scales):
    return unpack_weight(words.reshape(words.shape[0], 128, -1, 2), scales, "e2m1")


def planes(Y):
    n, m = Y.shape
    b = f64(bf(Y)).reshape(n // 32, 32, m)
    amax = np.abs(b).max(1)
    byte = np.clip(np.where(amax > 0, np.frexp(amax)[1] - 1 + 127 - 7, 1), 1, 254)
    codes = (b * np.exp2(127.0 - byte)[:, None, :]).reshape(n, m).astype(np.float32).astype(ml_dtypes.float8_e4m3fn).view(np.uint8)
    words = codes.reshape(n // 512, 128, 4, m).transpose(0, 1, 3, 2)
    return np.ascontiguousarray(words), np.ascontiguousarray(byte.astype(np.uint8).reshape(n // 512, 16, m))


MEMBERS, TRACERS, CELLS = 8, 128, 2048


def setup_inputs():
    s = mx_kscale(CELLS)
    spread = np.exp(0.8 * np.random.randn(CELLS))
    x = np.random.randn(CELLS, MEMBERS * TRACERS)
    x_words, x_scales = pack_weight(x * s[:, None], "e4m3")
    advect = np.random.randn(CELLS, CELLS) / np.sqrt(CELLS) * spread[None, :]
    rate = 0.1 + 0.8 * np.random.rand(TRACERS)
    source = 0.4 * np.random.randn(TRACERS, CELLS) * spread[None, :]
    return {
        "x_words": x_words,
        "x_scales": x_scales,
        "advect": bf(advect / s[:, None]),
        "rate": bf(rate),
        "source": bf(source),
    }

def reference(x_words, x_scales, advect, rate, source):
    X = unpack_weight(x_words, x_scales, "e4m3")
    A = mxq(f64(advect), 0, "e4m3")
    flow = (X.T @ A).reshape(MEMBERS, TRACERS, CELLS)
    y = flow * np.exp(-f64(rate))[None, :, None] + f64(source)[None, :, :]
    Y = y.reshape(MEMBERS * TRACERS, CELLS).T
    words, scales = planes(Y)
    return y, words, scales

@@ -1,0 +1,352 @@
+from contextlib import ExitStack
+
+import concourse.mybir as mybir
+from concourse.masks import make_identity
+
+F32 = mybir.dt.float32
+BF16 = mybir.dt.bfloat16
+I32 = mybir.dt.int32
+U32 = mybir.dt.uint32
+U8 = mybir.dt.uint8
+FP8X4 = mybir.dt.float8_e4m3fn_x4
+ALU = mybir.AluOpType
+ACT = mybir.ActivationFunctionType
+
+P = 128
+PACK = 4
+MEMBERS = 8
+CELLS = 2048
+ROWS = MEMBERS * P
+WIDTH = 512
+CHUNKS = CELLS // WIDTH
+PASSES = CELLS // (P * PACK)
+PAIRS = MEMBERS // 2
+FLOPS = 2 * ROWS * CELLS * CELLS
+
+PIECES = [(c, g) for c in range(CHUNKS) for g in range(PASSES)]
+QUADS = [(c, first) for c in range(CHUNKS) for first in (0, 4)]
+RAW_SLOTS = 10
+MIXED_SLOTS = 4
+ROUNDED_SLOTS = 8
+TURNED_SLOTS = 4
+HEAD_SHARE = 288
+SECOND_SHARE = 256
+USE_G = 1
+MID_SHARE = 0
+LATE_SHARE = 0
+
+
+def tile_tracer_advect_decay_source_g6_kernel(
+    tc, x_words, x_scales, advect, rate, source, out_0, out_1, out_2
+):
+    nc = tc.nc
+    with ExitStack() as ctx:
+        sb = ctx.enter_context(tc.tile_pool(name="sb", bufs=1))
+        ps = ctx.enter_context(tc.psum_pool(name="ps", bufs=1))
+        ctx.enter_context(tc.manual_schedule())
+
+        def tiles(name, count, shape, dtype):
+            return [sb.tile(shape, dtype, name="%s%d" % (name, i), align_bytes=64) for i in range(count)]
+
+        banks = [ps.tile([P, WIDTH], F32, name="bank%d" % i) for i in range(8)]
+        x_low = tiles("x_low", PASSES, [P, 4 * P], U32)
+        x_high = tiles("x_high", 2, [P, PASSES, 2 * P], U32)
+        x_plane = sb.tile([P, ROWS], U8, name="x_plane", align_bytes=64)
+        a_raw = tiles("a_raw", RAW_SLOTS, [P, PACK, WIDTH], BF16)
+        a_mixed = tiles("a_mixed", MIXED_SLOTS, [P, WIDTH, PACK], BF16)
+        a_codes = tiles("a_codes", CHUNKS * PASSES, [P, WIDTH], U32)
+        a_plane = tiles("a_plane", CHUNKS * PASSES, [P, WIDTH], U8)
+        src = tiles("src", CHUNKS, [P, WIDTH], BF16)
+        rate_col = sb.tile([P, 1], BF16, name="rate_col")
+        decay = sb.tile([P, 1], F32, name="decay")
+        ident = sb.tile([P, P], F32, name="ident")
+        y = tiles("y", CHUNKS * PAIRS, [P, 2, WIDTH], F32)
+        rounded = tiles("rounded", ROUNDED_SLOTS, [P, 2 * WIDTH], BF16)
+        turned = tiles("turned", TURNED_SLOTS, [P, 4 * P * PACK], BF16)
+        y_codes = tiles("y_codes", CHUNKS, [P, ROWS], U32)
+        y_plane = sb.tile([P, ROWS], U8, name="y_plane", align_bytes=64)
+
+        def load_a(piece):
+            chunk, g = PIECES[piece]
+            rows = advect[g * 512 : (g + 1) * 512, chunk * WIDTH : (chunk + 1) * WIDTH]
+            nc.sync.dma_start(out=a_raw[piece % RAW_SLOTS][:], in_=rows.rearrange("(p t) c -> p t c", t=PACK))
+
+        def load_x_low(g):
+            words = x_words[g].rearrange("p n t -> p (n t)").bitcast(I32)
+            nc.sync.dma_start(out=x_low[g][:].bitcast(I32), in_=words[:, : 4 * P])
+
+        def load_x_high(pair):
+            words = x_words.rearrange("g p n t -> p g (n t)").bitcast(I32)
+            cols = slice((4 + 2 * pair) * P, (6 + 2 * pair) * P)
+            nc.sync.dma_start(out=x_high[pair][:].bitcast(I32), in_=words[:, :, cols])
+
+        def x_operand(g, member):
+            if member < 4:
+                return x_low[g][:, member * P : (member + 1) * P]
+            return x_high[member // 2 - 2][:, g, (member % 2) * P : (member % 2 + 1) * P]
+
+        def load_src(chunk):
+            nc.sync.dma_start(out=src[chunk][:], in_=source[:, chunk * WIDTH : (chunk + 1) * WIDTH])
+
+        def interleave(piece, vector_cols):
+            raw, mixed = a_raw[piece % RAW_SLOTS], a_mixed[piece % MIXED_SLOTS]
+            for copy, lo, hi in ((nc.vector.tensor_copy, 0, vector_cols), (nc.scalar.copy, vector_cols, WIDTH)):
+                if hi > lo:
+                    copy(
+                        out=mixed[:, lo:hi, :].rearrange("p (c i) t -> p c t i", i=4),
+                        in_=raw[:, :, lo:hi].rearrange("p t (c i) -> p c t i", i=4),
+                    )
+            if piece + RAW_SLOTS < CHUNKS * PASSES:
+                load_a(piece + RAW_SLOTS)
+
+        def quantize_a(piece):
+            nc.vector.quantize_mx(
+                out=a_codes[piece][:].bitcast(FP8X4),
+                scales=a_plane[piece][:],
+                in_=a_mixed[piece % MIXED_SLOTS][:].rearrange("p c t -> p (c t)"),
+            )
+
+        def multiply(chunk, member, bank, passes):
+            cols = slice(member * P, (member + 1) * P)
+            for g in passes:
+                piece = PIECES.index((chunk, g))
+                nc.tensor.matmul_mx(
+                    out=banks[bank][:],
+                    lhsT=x_operand(g, member).bitcast(FP8X4),
+                    lhsT_scale=x_plane[4 * g :, cols],
+                    rhs=a_codes[piece][:].bitcast(FP8X4),
+                    rhs_scale=a_plane[piece][:],
+                    start=(g == 0),
+                    stop=(g == PASSES - 1),
+                )
+
+        def finish(chunk, member, bank):
+            nc.vector.scalar_tensor_tensor(
+                out=y[chunk * PAIRS + member // 2][:, member % 2, :],
+                in0=banks[bank][:],
+                scalar=decay[:],
+                in1=src[chunk][:],
+                op0=ALU.mult,
+                op1=ALU.add,
+            )
+
+        def store_y(chunk, first, count):
+            tile_y = y[chunk * PAIRS + first // 2][:, first % 2 : first % 2 + count, :]
+            rows = out_0[first : first + count, :, chunk * WIDTH : (chunk + 1) * WIDTH]
+            nc.sync.dma_start(out=rows.rearrange("e r c -> r e c"), in_=tile_y)
+
+        def rounded_slot(chunk, first):
+            return (2 * QUADS.index((chunk, first // 4 * 4)) + first % 4 // 2) % ROUNDED_SLOTS
+
+        def round_y(copy, chunk, first, count):
+            pair = chunk * PAIRS + first // 2
+            lo, hi = first % 2, first % 2 + count
+            copy(
+                out=rounded[rounded_slot(chunk, first)][:, lo * WIDTH : hi * WIDTH].rearrange(
+                    "r (m u p e) -> r m u p e", u=2, p=P, e=2
+                ),
+                in_=y[pair][:, lo:hi, :].rearrange("r m (p u e) -> r m u p e", u=2, e=2),
+            )
+
+        def turn(chunk, first, count, bank):
+            words = rounded[rounded_slot(chunk, first)][:].bitcast(F32)
+            for slot in range(2 * (first % 2), 2 * (first % 2 + count)):
+                cols = slice(slot * P, (slot + 1) * P)
+                nc.tensor.transpose(banks[bank][:, cols], words[:, cols], ident[:])
+
+        def collect(copy, chunk, first, count, bank):
+            half = turned[QUADS.index((chunk, first // 4 * 4)) % TURNED_SLOTS][:].bitcast(F32)
+            lo = 2 * P * (first % 4)
+            plo = 2 * P * (first % 2)
+            copy(
+                out=half[:, lo : lo + 2 * P * count].rearrange("p (m r u) -> p m r u", r=P, u=2),
+                in_=banks[bank][:, plo : plo + 2 * P * count].rearrange("p (m u r) -> p m r u", u=2, r=P),
+            )
+
+        def quantize_y(chunk, first, count):
+            cols = slice(first * P, (first + count) * P)
+            lo = (first % 4) * P * PACK
+            nc.vector.quantize_mx(
+                out=y_codes[chunk][:, cols].bitcast(FP8X4),
+                scales=y_plane[4 * chunk :, cols],
+                in_=turned[QUADS.index((chunk, first // 4 * 4)) % TURNED_SLOTS][:, lo : lo + count * P * PACK],
+            )
+
+        def store_codes(chunk, first, count):
+            cols = slice(first * P, (first + count) * P)
+            words = out_1[chunk].rearrange("p n t -> p (n t)").bitcast(I32)
+            nc.sync.dma_start(out=words[:, cols], in_=y_codes[chunk][:, cols].bitcast(I32))
+
+        v_copy, s_copy = nc.vector.tensor_copy, nc.scalar.copy
+
+        def g_copy(out, in_):
+            nc.gpsimd.tensor_scalar(out=out, in0=in_, scalar1=1.0, scalar2=0.0, op0=ALU.mult, op1=ALU.subtract)
+
+        nc.scalar.dma_start(out=rate_col[:], in_=rate.rearrange("(p o) -> p o", o=1))
+        nc.vector.memset(x_plane[:].bitcast(I32), 0)
+        load_a(0)
+        for q in range(4):
+            nc.sync.dma_start(
+                out=x_plane[32 * q : 32 * q + 16, :].bitcast(I32),
+                in_=x_scales[:, 4 * q : 4 * q + 4, :].bitcast(I32),
+            )
+        load_x_low(0)
+        load_a(1)
+        load_x_low(1)
+        load_a(2)
+        load_a(3)
+        load_x_low(2)
+        load_x_low(3)
+        load_src(0)
+        load_x_high(0)
+        load_x_high(1)
+        for piece in range(4, 8):
+            load_a(piece)
+        load_src(1)
+        load_a(8)
+        load_a(9)
+        nc.scalar.activation(out=decay[:], in_=rate_col[:], func=ACT.Exp, scale=-1.0)
+        make_identity(nc, ident[:])
+
+        def sweep(chunk, g):
+            for member in range(4):
+                multiply(chunk, member, member, [g])
+
+        def whole(chunk, member):
+            multiply(chunk, member, member, range(PASSES))
+
+        def leave_quad(chunk, first, first_pair_copy):
+            for member in range(first, first + 4):
+                finish(chunk, member, member)
+                if member % 2 == 1:
+                    store_y(chunk, member - 1, 2)
+                if member == first + 1:
+                    for half in range(2 if first_pair_copy is g_copy else 1):
+                        if first_pair_copy is g_copy:
+                            round_y(g_copy, chunk, first + half, 1)
+                        else:
+                            round_y(first_pair_copy, chunk, first, 2)
+
+        def turn_chunk(chunk, banks_from):
+            for pair in range(PAIRS):
+                turn(chunk, 2 * pair, 2, banks_from + pair)
+
+        def collect_chunk(chunk, banks_from):
+            for pair in range(PAIRS):
+                collect(s_copy, chunk, 2 * pair, 2, banks_from + pair)
+
+        def planes(chunk, first):
+            quantize_y(chunk, first, 4)
+            store_codes(chunk, first, 4)
+
+        gv = g_copy if USE_G else v_copy
+
+        for g in range(PASSES):
+            interleave(g, HEAD_SHARE)
+            quantize_a(g)
+            sweep(0, g)
+            if g == 1:
+                load_src(2)
+        load_src(3)
+        for member in range(4, 8):
+            whole(0, member)
+        for member in range(4):
+            finish(0, member, member)
+            if member == 1:
+                round_y(gv, 0, 0, 1)
+                round_y(gv, 0, 1, 1)
+        interleave(4, SECOND_SHARE)
+        for g in range(PASSES):
+            if g < PASSES - 1:
+                interleave(5 + g, SECOND_SHARE)
+            quantize_a(4 + g)
+            sweep(1, g)
+        store_y(0, 0, 2)
+        store_y(0, 2, 2)
+        interleave(8, MID_SHARE)
+        leave_quad(0, 4, gv)
+        for member in range(4, 8):
+            whole(1, member)
+        interleave(9, MID_SHARE)
+        quantize_a(8)
+        leave_quad(1, 0, gv)
+        interleave(10, MID_SHARE)
+        quantize_a(9)
+        round_y(v_copy, 0, 2, 2)
+        round_y(v_copy, 0, 6, 2)
+        interleave(11, MID_SHARE)
+        quantize_a(10)
+        for g in range(3):
+            sweep(2, g)
+        leave_quad(1, 4, gv)
+        turn_chunk(0, 4)
+        interleave(12, LATE_SHARE)
+        quantize_a(11)
+        sweep(2, 3)
+        round_y(v_copy, 1, 2, 2)
+        round_y(v_copy, 1, 6, 2)
+        collect_chunk(0, 4)
+        quantize_a(12)
+        whole(2, 4)
+        whole(2, 5)
+        interleave(13, LATE_SHARE)
+        leave_quad(2, 0, gv)
+        turn_chunk(1, 0)
+        whole(2, 6)
+        whole(2, 7)
+        planes(0, 0)
+        planes(0, 4)
+        collect_chunk(1, 0)
+        interleave(14, LATE_SHARE)
+        quantize_a(13)
+        round_y(v_copy, 2, 2, 2)
+        planes(1, 0)
+        sweep(3, 0)
+        sweep(3, 1)
+        leave_quad(2, 4, gv)
+        interleave(15, LATE_SHARE)
+        quantize_a(14)
+        round_y(v_copy, 2, 6, 2)
+        sweep(3, 2)
+        turn_chunk(2, 4)
+        planes(1, 4)
+        quantize_a(15)
+        sweep(3, 3)
+        collect_chunk(2, 4)
+        planes(2, 0)
+        whole(3, 4)
+        whole(3, 5)
+        leave_quad(3, 0, gv)
+        round_y(s_copy, 3, 2, 2)
+        whole(3, 6)
+        finish(3, 4, 4)
+        finish(3, 5, 5)
+        store_y(3, 4, 2)
+        round_y(s_copy, 3, 4, 2)
+        planes(2, 4)
+        turn(3, 0, 2, 0)
+        turn(3, 2, 2, 1)
+        whole(3, 7)
+        finish(3, 6, 6)
+        store_y(3, 6, 1)
+        collect(s_copy, 3, 0, 2, 0)
+        collect(s_copy, 3, 2, 2, 1)
+        round_y(v_copy, 3, 6, 1)
+        turn(3, 4, 2, 2)
+        turn(3, 6, 1, 3)
+        finish(3, 7, 7)
+        store_y(3, 7, 1)
+        round_y(v_copy, 3, 7, 1)
+        collect(s_copy, 3, 4, 2, 2)
+        collect(s_copy, 3, 6, 1, 3)
+        planes(3, 0)
+        turn(3, 7, 1, 0)
+        quantize_y(3, 4, 2)
+        collect(s_copy, 3, 7, 1, 0)
+        quantize_y(3, 6, 2)
+        store_codes(3, 4, 4)
+        for q in range(4):
+            nc.scalar.dma_start(
+                out=out_2[:, 4 * q : 4 * q + 4, :].bitcast(I32),
+                in_=y_plane[32 * q : 32 * q + 16, :].bitcast(I32),
+            )

@@ -130,6 +130,19 @@ def tile_tracer_advect_decay_source_g6_kernel(
                 op1=ALU.add,
             )
 
+        def finish_rounded(chunk, member, bank):
+            lo = (member % 2) * WIDTH
+            words = rounded[rounded_slot(chunk, member)][:, lo : lo + WIDTH].rearrange("r (u p e) -> r u p e", u=2, e=2)
+            for u in range(2):
+                nc.vector.scalar_tensor_tensor(
+                    out=words[:, u],
+                    in0=banks[bank][:].rearrange("r (p u e) -> r u p e", u=2, e=2)[:, u],
+                    scalar=decay[:],
+                    in1=src[chunk][:].rearrange("r (p u e) -> r u p e", u=2, e=2)[:, u],
+                    op0=ALU.mult,
+                    op1=ALU.add,
+                )
+
         def store_y(chunk, first, count):
             tile_y = y[chunk * PAIRS + first // 2][:, first % 2 : first % 2 + count, :]
             rows = out_0[first : first + count, :, chunk * WIDTH : (chunk + 1) * WIDTH]
@@ -180,7 +193,7 @@ def tile_tracer_advect_decay_source_g6_kernel(
         v_copy, s_copy = nc.vector.tensor_copy, nc.scalar.copy
 
         def g_copy(out, in_):
-            nc.gpsimd.tensor_scalar(out=out, in0=in_, scalar1=1.0, scalar2=0.0, op0=ALU.mult, op1=ALU.subtract)
+            nc.gpsimd.tensor_scalar(out=out, in0=in_, scalar1=1.0, scalar2=1.0, op0=ALU.mult, op1=ALU.mult)
 
         nc.scalar.dma_start(out=rate_col[:], in_=rate.rearrange("(p o) -> p o", o=1))
         nc.vector.memset(x_plane[:].bitcast(I32), 0)
@@ -319,11 +332,12 @@ def tile_tracer_advect_decay_source_g6_kernel(
         leave_quad(3, 0, gv)
         round_y(s_copy, 3, 2, 2)
         whole(3, 6)
-        finish(3, 4, 4)
-        finish(3, 5, 5)
-        store_y(3, 4, 2)
-        round_y(s_copy, 3, 4, 2)
         planes(2, 4)
+        finish(3, 4, 4)
+        round_y(gv, 3, 4, 1)
+        finish(3, 5, 5)
+        round_y(gv, 3, 5, 1)
+        store_y(3, 4, 2)
         turn(3, 0, 2, 0)
         turn(3, 2, 2, 1)
         whole(3, 7)
@@ -331,22 +345,23 @@ def tile_tracer_advect_decay_source_g6_kernel(
         store_y(3, 6, 1)
         collect(s_copy, 3, 0, 2, 0)
         collect(s_copy, 3, 2, 2, 1)
-        round_y(v_copy, 3, 6, 1)
+        round_y(s_copy, 3, 6, 1)
+        planes(3, 0)
         turn(3, 4, 2, 2)
         turn(3, 6, 1, 3)
-        finish(3, 7, 7)
-        store_y(3, 7, 1)
-        round_y(v_copy, 3, 7, 1)
+        finish_rounded(3, 7, 7)
         collect(s_copy, 3, 4, 2, 2)
         collect(s_copy, 3, 6, 1, 3)
-        planes(3, 0)
         turn(3, 7, 1, 0)
+        finish(3, 7, 7)
+        store_y(3, 7, 1)
         quantize_y(3, 4, 2)
+        store_codes(3, 4, 2)
         collect(s_copy, 3, 7, 1, 0)
         quantize_y(3, 6, 2)
-        store_codes(3, 4, 4)
+        store_codes(3, 6, 2)
         for q in range(4):
-            nc.scalar.dma_start(
+            (nc.sync, nc.scalar)[q % 2].dma_start(
                 out=out_2[:, 4 * q : 4 * q + 4, :].bitcast(I32),
                 in_=y_plane[32 * q : 32 * q + 16, :].bitcast(I32),
             )

@@ -31,9 +31,8 @@ ROUNDED_SLOTS = 8
 TURNED_SLOTS = 4
 HEAD_SHARE = 288
 SECOND_SHARE = 256
-USE_G = 1
 MID_SHARE = 0
-LATE_SHARE = 0
+LATE_SHARE = 128
 
 
 def tile_tracer_advect_decay_source_g6_kernel(
@@ -192,9 +191,6 @@ def tile_tracer_advect_decay_source_g6_kernel(
 
         v_copy, s_copy = nc.vector.tensor_copy, nc.scalar.copy
 
-        def g_copy(out, in_):
-            nc.gpsimd.tensor_scalar(out=out, in0=in_, scalar1=1.0, scalar2=1.0, op0=ALU.mult, op1=ALU.mult)
-
         nc.scalar.dma_start(out=rate_col[:], in_=rate.rearrange("(p o) -> p o", o=1))
         nc.vector.memset(x_plane[:].bitcast(I32), 0)
         load_a(0)
@@ -212,8 +208,9 @@ def tile_tracer_advect_decay_source_g6_kernel(
         load_x_low(3)
         load_src(0)
         load_x_high(0)
+        load_a(4)
         load_x_high(1)
-        for piece in range(4, 8):
+        for piece in range(5, 8):
             load_a(piece)
         load_src(1)
         load_a(8)
@@ -228,17 +225,23 @@ def tile_tracer_advect_decay_source_g6_kernel(
         def whole(chunk, member):
             multiply(chunk, member, member, range(PASSES))
 
-        def leave_quad(chunk, first, first_pair_copy):
+        def leave_quad(chunk, first):
             for member in range(first, first + 4):
                 finish(chunk, member, member)
                 if member % 2 == 1:
                     store_y(chunk, member - 1, 2)
-                if member == first + 1:
-                    for half in range(2 if first_pair_copy is g_copy else 1):
-                        if first_pair_copy is g_copy:
-                            round_y(g_copy, chunk, first + half, 1)
-                        else:
-                            round_y(first_pair_copy, chunk, first, 2)
+
+        def turn_quad(chunk, first, bank):
+            turn(chunk, first, 2, bank)
+            turn(chunk, first + 2, 2, bank + 1)
+
+        def collect_quad(chunk, first, bank):
+            collect(s_copy, chunk, first, 2, bank)
+            collect(s_copy, chunk, first + 2, 2, bank + 1)
+
+        def round_quad(copy, chunk, first):
+            round_y(copy, chunk, first, 2)
+            round_y(copy, chunk, first + 2, 2)
 
         def turn_chunk(chunk, banks_from):
             for pair in range(PAIRS):
@@ -252,8 +255,6 @@ def tile_tracer_advect_decay_source_g6_kernel(
             quantize_y(chunk, first, 4)
             store_codes(chunk, first, 4)
 
-        gv = g_copy if USE_G else v_copy
-
         for g in range(PASSES):
             interleave(g, HEAD_SHARE)
             quantize_a(g)
@@ -263,12 +264,10 @@ def tile_tracer_advect_decay_source_g6_kernel(
         load_src(3)
         for member in range(4, 8):
             whole(0, member)
+        interleave(4, 0)
         for member in range(4):
             finish(0, member, member)
-            if member == 1:
-                round_y(gv, 0, 0, 1)
-                round_y(gv, 0, 1, 1)
-        interleave(4, SECOND_SHARE)
+        round_y(v_copy, 0, 0, 2)
         for g in range(PASSES):
             if g < PASSES - 1:
                 interleave(5 + g, SECOND_SHARE)
@@ -277,87 +276,88 @@ def tile_tracer_advect_decay_source_g6_kernel(
         store_y(0, 0, 2)
         store_y(0, 2, 2)
         interleave(8, MID_SHARE)
-        leave_quad(0, 4, gv)
+        leave_quad(0, 4)
         for member in range(4, 8):
             whole(1, member)
         interleave(9, MID_SHARE)
         quantize_a(8)
-        leave_quad(1, 0, gv)
+        leave_quad(1, 0)
         interleave(10, MID_SHARE)
         quantize_a(9)
         round_y(v_copy, 0, 2, 2)
-        round_y(v_copy, 0, 6, 2)
+        round_y(v_copy, 0, 4, 2)
         interleave(11, MID_SHARE)
         quantize_a(10)
         for g in range(3):
             sweep(2, g)
-        leave_quad(1, 4, gv)
-        turn_chunk(0, 4)
-        interleave(12, LATE_SHARE)
+        leave_quad(1, 4)
+        interleave(12, MID_SHARE)
         quantize_a(11)
         sweep(2, 3)
-        round_y(v_copy, 1, 2, 2)
-        round_y(v_copy, 1, 6, 2)
+        round_y(v_copy, 0, 6, 2)
+        turn_chunk(0, 4)
+        round_y(s_copy, 1, 0, 2)
         collect_chunk(0, 4)
         quantize_a(12)
+        leave_quad(2, 0)
         whole(2, 4)
         whole(2, 5)
         interleave(13, LATE_SHARE)
-        leave_quad(2, 0, gv)
-        turn_chunk(1, 0)
+        round_y(v_copy, 1, 2, 2)
+        round_quad(v_copy, 1, 4)
         whole(2, 6)
+        turn_chunk(1, 0)
         whole(2, 7)
+        interleave(14, LATE_SHARE)
+        quantize_a(13)
         planes(0, 0)
         planes(0, 4)
         collect_chunk(1, 0)
-        interleave(14, LATE_SHARE)
-        quantize_a(13)
-        round_y(v_copy, 2, 2, 2)
-        planes(1, 0)
         sweep(3, 0)
         sweep(3, 1)
-        leave_quad(2, 4, gv)
-        interleave(15, LATE_SHARE)
         quantize_a(14)
-        round_y(v_copy, 2, 6, 2)
+        interleave(15, LATE_SHARE)
+        leave_quad(2, 4)
+        round_quad(v_copy, 2, 0)
         sweep(3, 2)
-        turn_chunk(2, 4)
-        planes(1, 4)
+        turn_quad(2, 0, 4)
         quantize_a(15)
         sweep(3, 3)
-        collect_chunk(2, 4)
-        planes(2, 0)
+        planes(1, 0)
+        planes(1, 4)
+        round_quad(s_copy, 2, 4)
+        turn_quad(2, 4, 6)
+        collect_quad(2, 0, 4)
+        collect_quad(2, 4, 6)
         whole(3, 4)
         whole(3, 5)
-        leave_quad(3, 0, gv)
-        round_y(s_copy, 3, 2, 2)
+        leave_quad(3, 0)
+        round_quad(s_copy, 3, 0)
         whole(3, 6)
-        planes(2, 4)
+        planes(2, 0)
         finish(3, 4, 4)
-        round_y(gv, 3, 4, 1)
+        planes(2, 4)
         finish(3, 5, 5)
-        round_y(gv, 3, 5, 1)
         store_y(3, 4, 2)
-        turn(3, 0, 2, 0)
-        turn(3, 2, 2, 1)
+        turn_quad(3, 0, 2)
         whole(3, 7)
+        round_y(v_copy, 3, 4, 2)
         finish(3, 6, 6)
         store_y(3, 6, 1)
-        collect(s_copy, 3, 0, 2, 0)
-        collect(s_copy, 3, 2, 2, 1)
-        round_y(s_copy, 3, 6, 1)
+        collect_quad(3, 0, 2)
+        round_y(v_copy, 3, 6, 1)
         planes(3, 0)
-        turn(3, 4, 2, 2)
-        turn(3, 6, 1, 3)
+        turn(3, 4, 2, 4)
+        turn(3, 6, 1, 5)
         finish_rounded(3, 7, 7)
-        collect(s_copy, 3, 4, 2, 2)
-        collect(s_copy, 3, 6, 1, 3)
-        turn(3, 7, 1, 0)
+        collect(s_copy, 3, 4, 2, 4)
+        collect(s_copy, 3, 6, 1, 5)
+        turn(3, 7, 1, 6)
         finish(3, 7, 7)
         store_y(3, 7, 1)
         quantize_y(3, 4, 2)
         store_codes(3, 4, 2)
-        collect(s_copy, 3, 7, 1, 0)
+        collect(s_copy, 3, 7, 1, 6)
         quantize_y(3, 6, 2)
         store_codes(3, 6, 2)
         for q in range(4):

@@ -14,25 +14,28 @@ ACT = mybir.ActivationFunctionType
 
 P = 128
 PACK = 4
+K_PASS = P * PACK
 MEMBERS = 8
+QUAD = 4
 CELLS = 2048
 ROWS = MEMBERS * P
 WIDTH = 512
 CHUNKS = CELLS // WIDTH
-PASSES = CELLS // (P * PACK)
+PASSES = CELLS // K_PASS
+PIECES = CHUNKS * PASSES
 PAIRS = MEMBERS // 2
+BANKS = 8
+QUADRANTS = 4
 FLOPS = 2 * ROWS * CELLS * CELLS
 
-PIECES = [(c, g) for c in range(CHUNKS) for g in range(PASSES)]
-QUADS = [(c, first) for c in range(CHUNKS) for first in (0, 4)]
 RAW_SLOTS = 10
 MIXED_SLOTS = 4
 ROUNDED_SLOTS = 8
 TURNED_SLOTS = 4
-HEAD_SHARE = 288
-SECOND_SHARE = 256
-MID_SHARE = 0
-LATE_SHARE = 128
+
+CHUNK0_SHARE = 288
+CHUNK1_SHARE = 256
+CHUNK3_SHARE = 128
 
 
 def tile_tracer_advect_decay_source_g6_kernel(
@@ -47,162 +50,188 @@ def tile_tracer_advect_decay_source_g6_kernel(
         def tiles(name, count, shape, dtype):
             return [sb.tile(shape, dtype, name="%s%d" % (name, i), align_bytes=64) for i in range(count)]
 
-        banks = [ps.tile([P, WIDTH], F32, name="bank%d" % i) for i in range(8)]
-        x_low = tiles("x_low", PASSES, [P, 4 * P], U32)
+        banks = [ps.tile([P, WIDTH], F32, name="bank%d" % i) for i in range(BANKS)]
+        x_low = tiles("x_low", PASSES, [P, QUAD * P], U32)
         x_high = tiles("x_high", 2, [P, PASSES, 2 * P], U32)
         x_plane = sb.tile([P, ROWS], U8, name="x_plane", align_bytes=64)
         a_raw = tiles("a_raw", RAW_SLOTS, [P, PACK, WIDTH], BF16)
         a_mixed = tiles("a_mixed", MIXED_SLOTS, [P, WIDTH, PACK], BF16)
-        a_codes = tiles("a_codes", CHUNKS * PASSES, [P, WIDTH], U32)
-        a_plane = tiles("a_plane", CHUNKS * PASSES, [P, WIDTH], U8)
+        a_codes = tiles("a_codes", PIECES, [P, WIDTH], U32)
+        a_plane = tiles("a_plane", PIECES, [P, WIDTH], U8)
         src = tiles("src", CHUNKS, [P, WIDTH], BF16)
         rate_col = sb.tile([P, 1], BF16, name="rate_col")
         decay = sb.tile([P, 1], F32, name="decay")
         ident = sb.tile([P, P], F32, name="ident")
         y = tiles("y", CHUNKS * PAIRS, [P, 2, WIDTH], F32)
         rounded = tiles("rounded", ROUNDED_SLOTS, [P, 2 * WIDTH], BF16)
-        turned = tiles("turned", TURNED_SLOTS, [P, 4 * P * PACK], BF16)
+        turned = tiles("turned", TURNED_SLOTS, [P, QUAD * P * PACK], BF16)
         y_codes = tiles("y_codes", CHUNKS, [P, ROWS], U32)
         y_plane = sb.tile([P, ROWS], U8, name="y_plane", align_bytes=64)
 
+        vector_copy, scalar_copy = nc.vector.tensor_copy, nc.scalar.copy
+
+
         def load_a(piece):
-            chunk, g = PIECES[piece]
-            rows = advect[g * 512 : (g + 1) * 512, chunk * WIDTH : (chunk + 1) * WIDTH]
+            chunk, g = divmod(piece, PASSES)
+            rows = advect[g * K_PASS : (g + 1) * K_PASS, chunk * WIDTH : (chunk + 1) * WIDTH]
             nc.sync.dma_start(out=a_raw[piece % RAW_SLOTS][:], in_=rows.rearrange("(p t) c -> p t c", t=PACK))
 
         def load_x_low(g):
             words = x_words[g].rearrange("p n t -> p (n t)").bitcast(I32)
-            nc.sync.dma_start(out=x_low[g][:].bitcast(I32), in_=words[:, : 4 * P])
+            nc.sync.dma_start(out=x_low[g][:].bitcast(I32), in_=words[:, : QUAD * P])
 
-        def load_x_high(pair):
+        def load_x_high(half):
             words = x_words.rearrange("g p n t -> p g (n t)").bitcast(I32)
-            cols = slice((4 + 2 * pair) * P, (6 + 2 * pair) * P)
-            nc.sync.dma_start(out=x_high[pair][:].bitcast(I32), in_=words[:, :, cols])
-
-        def x_operand(g, member):
-            if member < 4:
-                return x_low[g][:, member * P : (member + 1) * P]
-            return x_high[member // 2 - 2][:, g, (member % 2) * P : (member % 2 + 1) * P]
+            cols = slice((QUAD + 2 * half) * P, (QUAD + 2 * half + 2) * P)
+            nc.sync.dma_start(out=x_high[half][:].bitcast(I32), in_=words[:, :, cols])
 
         def load_src(chunk):
             nc.sync.dma_start(out=src[chunk][:], in_=source[:, chunk * WIDTH : (chunk + 1) * WIDTH])
 
-        def interleave(piece, vector_cols):
+
+        def interleave(chunk, g, vector_cols):
+            piece = chunk * PASSES + g
             raw, mixed = a_raw[piece % RAW_SLOTS], a_mixed[piece % MIXED_SLOTS]
-            for copy, lo, hi in ((nc.vector.tensor_copy, 0, vector_cols), (nc.scalar.copy, vector_cols, WIDTH)):
+            for copy, lo, hi in ((vector_copy, 0, vector_cols), (scalar_copy, vector_cols, WIDTH)):
                 if hi > lo:
                     copy(
                         out=mixed[:, lo:hi, :].rearrange("p (c i) t -> p c t i", i=4),
                         in_=raw[:, :, lo:hi].rearrange("p t (c i) -> p c t i", i=4),
                     )
-            if piece + RAW_SLOTS < CHUNKS * PASSES:
+            if piece + RAW_SLOTS < PIECES:
                 load_a(piece + RAW_SLOTS)
 
-        def quantize_a(piece):
+        def quantize_a(chunk, g):
+            piece = chunk * PASSES + g
             nc.vector.quantize_mx(
                 out=a_codes[piece][:].bitcast(FP8X4),
                 scales=a_plane[piece][:],
                 in_=a_mixed[piece % MIXED_SLOTS][:].rearrange("p c t -> p (c t)"),
             )
 
-        def multiply(chunk, member, bank, passes):
-            cols = slice(member * P, (member + 1) * P)
-            for g in passes:
-                piece = PIECES.index((chunk, g))
-                nc.tensor.matmul_mx(
-                    out=banks[bank][:],
-                    lhsT=x_operand(g, member).bitcast(FP8X4),
-                    lhsT_scale=x_plane[4 * g :, cols],
-                    rhs=a_codes[piece][:].bitcast(FP8X4),
-                    rhs_scale=a_plane[piece][:],
-                    start=(g == 0),
-                    stop=(g == PASSES - 1),
-                )
+        def x_operand(g, member):
+            if member < QUAD:
+                return x_low[g][:, member * P : (member + 1) * P]
+            return x_high[(member - QUAD) // 2][:, g, (member % 2) * P : (member % 2 + 1) * P]
 
-        def finish(chunk, member, bank):
-            nc.vector.scalar_tensor_tensor(
-                out=y[chunk * PAIRS + member // 2][:, member % 2, :],
-                in0=banks[bank][:],
-                scalar=decay[:],
-                in1=src[chunk][:],
-                op0=ALU.mult,
-                op1=ALU.add,
+        def multiply(chunk, member, g):
+            piece = chunk * PASSES + g
+            nc.tensor.matmul_mx(
+                out=banks[member][:],
+                lhsT=x_operand(g, member).bitcast(FP8X4),
+                lhsT_scale=x_plane[4 * g :, member * P : (member + 1) * P],
+                rhs=a_codes[piece][:].bitcast(FP8X4),
+                rhs_scale=a_plane[piece][:],
+                start=(g == 0),
+                stop=(g == PASSES - 1),
             )
 
-        def finish_rounded(chunk, member, bank):
-            lo = (member % 2) * WIDTH
-            words = rounded[rounded_slot(chunk, member)][:, lo : lo + WIDTH].rearrange("r (u p e) -> r u p e", u=2, e=2)
-            for u in range(2):
-                nc.vector.scalar_tensor_tensor(
-                    out=words[:, u],
-                    in0=banks[bank][:].rearrange("r (p u e) -> r u p e", u=2, e=2)[:, u],
-                    scalar=decay[:],
-                    in1=src[chunk][:].rearrange("r (p u e) -> r u p e", u=2, e=2)[:, u],
-                    op0=ALU.mult,
-                    op1=ALU.add,
-                )
+        def sweep(chunk, g):
+            for member in range(QUAD):
+                multiply(chunk, member, g)
+
+        def whole(chunk, member):
+            for g in range(PASSES):
+                multiply(chunk, member, g)
+
+
+        def decay_and_source(out, flow, source_part):
+            nc.vector.scalar_tensor_tensor(
+                out=out, in0=flow, scalar=decay[:], in1=source_part, op0=ALU.mult, op1=ALU.add
+            )
+
+        def finish(chunk, member):
+            decay_and_source(y[chunk * PAIRS + member // 2][:, member % 2, :], banks[member][:], src[chunk][:])
 
         def store_y(chunk, first, count):
-            tile_y = y[chunk * PAIRS + first // 2][:, first % 2 : first % 2 + count, :]
+            part = y[chunk * PAIRS + first // 2][:, first % 2 : first % 2 + count, :]
             rows = out_0[first : first + count, :, chunk * WIDTH : (chunk + 1) * WIDTH]
-            nc.sync.dma_start(out=rows.rearrange("e r c -> r e c"), in_=tile_y)
+            nc.sync.dma_start(out=rows.rearrange("e r c -> r e c"), in_=part)
 
-        def rounded_slot(chunk, first):
-            return (2 * QUADS.index((chunk, first // 4 * 4)) + first % 4 // 2) % ROUNDED_SLOTS
+        def leave_pair(chunk, first):
+            finish(chunk, first)
+            finish(chunk, first + 1)
+            store_y(chunk, first, 2)
 
-        def round_y(copy, chunk, first, count):
-            pair = chunk * PAIRS + first // 2
+        def leave_quad(chunk, first):
+            leave_pair(chunk, first)
+            leave_pair(chunk, first + 2)
+
+
+        def rounded_tile(chunk, member):
+            return rounded[(chunk * PAIRS + member // 2) % ROUNDED_SLOTS]
+
+        def turned_tile(chunk, member):
+            return turned[(2 * chunk + member // QUAD) % TURNED_SLOTS]
+
+        def round_y(copy, chunk, first, count=2):
             lo, hi = first % 2, first % 2 + count
             copy(
-                out=rounded[rounded_slot(chunk, first)][:, lo * WIDTH : hi * WIDTH].rearrange(
+                out=rounded_tile(chunk, first)[:, lo * WIDTH : hi * WIDTH].rearrange(
                     "r (m u p e) -> r m u p e", u=2, p=P, e=2
                 ),
-                in_=y[pair][:, lo:hi, :].rearrange("r m (p u e) -> r m u p e", u=2, e=2),
+                in_=y[chunk * PAIRS + first // 2][:, lo:hi, :].rearrange("r m (p u e) -> r m u p e", u=2, e=2),
             )
 
-        def turn(chunk, first, count, bank):
-            words = rounded[rounded_slot(chunk, first)][:].bitcast(F32)
+        def round_quad(copy, chunk, first):
+            round_y(copy, chunk, first)
+            round_y(copy, chunk, first + 2)
+
+        def finish_rounded(chunk, member):
+            lo = (member % 2) * WIDTH
+            words = rounded_tile(chunk, member)[:, lo : lo + WIDTH].rearrange("r (u p e) -> r u p e", u=2, e=2)
+            flow = banks[member][:].rearrange("r (p u e) -> r u p e", u=2, e=2)
+            source_part = src[chunk][:].rearrange("r (p u e) -> r u p e", u=2, e=2)
+            for u in range(2):
+                decay_and_source(words[:, u], flow[:, u], source_part[:, u])
+
+        def turn(chunk, first, bank, count=2):
+            words = rounded_tile(chunk, first)[:].bitcast(F32)
             for slot in range(2 * (first % 2), 2 * (first % 2 + count)):
                 cols = slice(slot * P, (slot + 1) * P)
                 nc.tensor.transpose(banks[bank][:, cols], words[:, cols], ident[:])
 
-        def collect(copy, chunk, first, count, bank):
-            half = turned[QUADS.index((chunk, first // 4 * 4)) % TURNED_SLOTS][:].bitcast(F32)
-            lo = 2 * P * (first % 4)
-            plo = 2 * P * (first % 2)
-            copy(
-                out=half[:, lo : lo + 2 * P * count].rearrange("p (m r u) -> p m r u", r=P, u=2),
-                in_=banks[bank][:, plo : plo + 2 * P * count].rearrange("p (m u r) -> p m r u", u=2, r=P),
+        def collect(chunk, first, bank, count=2):
+            quad_words = turned_tile(chunk, first)[:].bitcast(F32)
+            to, frm, size = 2 * P * (first % QUAD), 2 * P * (first % 2), 2 * P * count
+            scalar_copy(
+                out=quad_words[:, to : to + size].rearrange("p (m r u) -> p m r u", r=P, u=2),
+                in_=banks[bank][:, frm : frm + size].rearrange("p (m u r) -> p m r u", u=2, r=P),
             )
 
-        def quantize_y(chunk, first, count):
+        def turn_pairs(chunk, pairs, first_bank):
+            for i, pair in enumerate(pairs):
+                turn(chunk, 2 * pair, first_bank + i)
+
+        def collect_pairs(chunk, pairs, first_bank):
+            for i, pair in enumerate(pairs):
+                collect(chunk, 2 * pair, first_bank + i)
+
+        def planes(chunk, first, count=QUAD):
             cols = slice(first * P, (first + count) * P)
-            lo = (first % 4) * P * PACK
+            lo = (first % QUAD) * K_PASS
             nc.vector.quantize_mx(
                 out=y_codes[chunk][:, cols].bitcast(FP8X4),
                 scales=y_plane[4 * chunk :, cols],
-                in_=turned[QUADS.index((chunk, first // 4 * 4)) % TURNED_SLOTS][:, lo : lo + count * P * PACK],
+                in_=turned_tile(chunk, first)[:, lo : lo + count * K_PASS],
             )
-
-        def store_codes(chunk, first, count):
-            cols = slice(first * P, (first + count) * P)
             words = out_1[chunk].rearrange("p n t -> p (n t)").bitcast(I32)
             nc.sync.dma_start(out=words[:, cols], in_=y_codes[chunk][:, cols].bitcast(I32))
 
-        v_copy, s_copy = nc.vector.tensor_copy, nc.scalar.copy
+        all_pairs, low_pairs, high_pairs = range(PAIRS), range(2), range(2, PAIRS)
 
         nc.scalar.dma_start(out=rate_col[:], in_=rate.rearrange("(p o) -> p o", o=1))
         nc.vector.memset(x_plane[:].bitcast(I32), 0)
         load_a(0)
-        for q in range(4):
+        for q in range(QUADRANTS):
             nc.sync.dma_start(
                 out=x_plane[32 * q : 32 * q + 16, :].bitcast(I32),
                 in_=x_scales[:, 4 * q : 4 * q + 4, :].bitcast(I32),
             )
         load_x_low(0)
         load_a(1)
-        load_x_low(1)
         load_a(2)
+        load_x_low(1)
         load_a(3)
         load_x_low(2)
         load_x_low(3)
@@ -218,149 +247,116 @@ def tile_tracer_advect_decay_source_g6_kernel(
         nc.scalar.activation(out=decay[:], in_=rate_col[:], func=ACT.Exp, scale=-1.0)
         make_identity(nc, ident[:])
 
-        def sweep(chunk, g):
-            for member in range(4):
-                multiply(chunk, member, member, [g])
-
-        def whole(chunk, member):
-            multiply(chunk, member, member, range(PASSES))
-
-        def leave_quad(chunk, first):
-            for member in range(first, first + 4):
-                finish(chunk, member, member)
-                if member % 2 == 1:
-                    store_y(chunk, member - 1, 2)
-
-        def turn_quad(chunk, first, bank):
-            turn(chunk, first, 2, bank)
-            turn(chunk, first + 2, 2, bank + 1)
-
-        def collect_quad(chunk, first, bank):
-            collect(s_copy, chunk, first, 2, bank)
-            collect(s_copy, chunk, first + 2, 2, bank + 1)
-
-        def round_quad(copy, chunk, first):
-            round_y(copy, chunk, first, 2)
-            round_y(copy, chunk, first + 2, 2)
-
-        def turn_chunk(chunk, banks_from):
-            for pair in range(PAIRS):
-                turn(chunk, 2 * pair, 2, banks_from + pair)
-
-        def collect_chunk(chunk, banks_from):
-            for pair in range(PAIRS):
-                collect(s_copy, chunk, 2 * pair, 2, banks_from + pair)
-
-        def planes(chunk, first):
-            quantize_y(chunk, first, 4)
-            store_codes(chunk, first, 4)
-
         for g in range(PASSES):
-            interleave(g, HEAD_SHARE)
-            quantize_a(g)
+            interleave(0, g, CHUNK0_SHARE)
+            quantize_a(0, g)
             sweep(0, g)
             if g == 1:
                 load_src(2)
         load_src(3)
-        for member in range(4, 8):
+        for member in range(QUAD, MEMBERS):
             whole(0, member)
-        interleave(4, 0)
-        for member in range(4):
-            finish(0, member, member)
-        round_y(v_copy, 0, 0, 2)
+
+        interleave(1, 0, 0)
+        for member in range(QUAD):
+            finish(0, member)
+        round_y(vector_copy, 0, 0)
         for g in range(PASSES):
             if g < PASSES - 1:
-                interleave(5 + g, SECOND_SHARE)
-            quantize_a(4 + g)
+                interleave(1, g + 1, CHUNK1_SHARE)
+            quantize_a(1, g)
             sweep(1, g)
         store_y(0, 0, 2)
         store_y(0, 2, 2)
-        interleave(8, MID_SHARE)
-        leave_quad(0, 4)
-        for member in range(4, 8):
+        interleave(2, 0, 0)
+        leave_quad(0, QUAD)
+        for member in range(QUAD, MEMBERS):
             whole(1, member)
-        interleave(9, MID_SHARE)
-        quantize_a(8)
+        interleave(2, 1, 0)
+        quantize_a(2, 0)
         leave_quad(1, 0)
-        interleave(10, MID_SHARE)
-        quantize_a(9)
-        round_y(v_copy, 0, 2, 2)
-        round_y(v_copy, 0, 4, 2)
-        interleave(11, MID_SHARE)
-        quantize_a(10)
-        for g in range(3):
+        interleave(2, 2, 0)
+        quantize_a(2, 1)
+        round_y(vector_copy, 0, 2)
+        round_y(vector_copy, 0, 4)
+        interleave(2, 3, 0)
+        quantize_a(2, 2)
+
+        for g in range(PASSES - 1):
             sweep(2, g)
-        leave_quad(1, 4)
-        interleave(12, MID_SHARE)
-        quantize_a(11)
+        leave_pair(1, 4)
+        interleave(3, 0, 0)
+        quantize_a(2, 3)
         sweep(2, 3)
-        round_y(v_copy, 0, 6, 2)
-        turn_chunk(0, 4)
-        round_y(s_copy, 1, 0, 2)
-        collect_chunk(0, 4)
-        quantize_a(12)
+        leave_pair(1, 6)
+        round_y(vector_copy, 0, 6)
+        turn_pairs(0, all_pairs, QUAD)
+        round_y(scalar_copy, 1, 0)
+        collect_pairs(0, all_pairs, QUAD)
+        quantize_a(3, 0)
         leave_quad(2, 0)
         whole(2, 4)
         whole(2, 5)
-        interleave(13, LATE_SHARE)
-        round_y(v_copy, 1, 2, 2)
-        round_quad(v_copy, 1, 4)
+        interleave(3, 1, CHUNK3_SHARE)
+        round_y(vector_copy, 1, 2)
+        round_quad(vector_copy, 1, QUAD)
         whole(2, 6)
-        turn_chunk(1, 0)
+        turn_pairs(1, all_pairs, 0)
         whole(2, 7)
-        interleave(14, LATE_SHARE)
-        quantize_a(13)
+        interleave(3, 2, CHUNK3_SHARE)
+        quantize_a(3, 1)
         planes(0, 0)
-        planes(0, 4)
-        collect_chunk(1, 0)
+        planes(0, QUAD)
+        collect_pairs(1, all_pairs, 0)
+
         sweep(3, 0)
         sweep(3, 1)
-        quantize_a(14)
-        interleave(15, LATE_SHARE)
-        leave_quad(2, 4)
-        round_quad(v_copy, 2, 0)
+        quantize_a(3, 2)
+        interleave(3, 3, CHUNK3_SHARE)
+        leave_quad(2, QUAD)
         sweep(3, 2)
-        turn_quad(2, 0, 4)
-        quantize_a(15)
+        round_y(vector_copy, 2, 0)
+        quantize_a(3, 3)
         sweep(3, 3)
+        round_y(vector_copy, 2, 2)
+        round_quad(scalar_copy, 2, QUAD)
+        turn_pairs(2, all_pairs, QUAD)
         planes(1, 0)
-        planes(1, 4)
-        round_quad(s_copy, 2, 4)
-        turn_quad(2, 4, 6)
-        collect_quad(2, 0, 4)
-        collect_quad(2, 4, 6)
+        collect_pairs(2, low_pairs, QUAD)
         whole(3, 4)
         whole(3, 5)
         leave_quad(3, 0)
-        round_quad(s_copy, 3, 0)
+        round_y(scalar_copy, 3, 0)
+        collect_pairs(2, high_pairs, QUAD + 2)
+        planes(1, QUAD)
+        round_y(vector_copy, 3, 2)
+        turn_pairs(3, low_pairs, 0)
         whole(3, 6)
-        planes(2, 0)
-        finish(3, 4, 4)
-        planes(2, 4)
-        finish(3, 5, 5)
-        store_y(3, 4, 2)
-        turn_quad(3, 0, 2)
         whole(3, 7)
-        round_y(v_copy, 3, 4, 2)
-        finish(3, 6, 6)
-        store_y(3, 6, 1)
-        collect_quad(3, 0, 2)
-        round_y(v_copy, 3, 6, 1)
+        planes(2, 0)
+        finish(3, 4)
+        planes(2, QUAD)
+        finish(3, 5)
+        store_y(3, 4, 2)
+        collect_pairs(3, low_pairs, 0)
+        round_y(scalar_copy, 3, 4)
         planes(3, 0)
-        turn(3, 4, 2, 4)
-        turn(3, 6, 1, 5)
-        finish_rounded(3, 7, 7)
-        collect(s_copy, 3, 4, 2, 4)
-        collect(s_copy, 3, 6, 1, 5)
-        turn(3, 7, 1, 6)
-        finish(3, 7, 7)
+
+        finish(3, 6)
+        store_y(3, 6, 1)
+        round_y(scalar_copy, 3, 6, 1)
+        turn(3, 4, 2)
+        turn(3, 6, 3, 1)
+        finish_rounded(3, 7)
+        collect(3, 4, 2)
+        collect(3, 6, 3, 1)
+        turn(3, 7, 0, 1)
+        finish(3, 7)
         store_y(3, 7, 1)
-        quantize_y(3, 4, 2)
-        store_codes(3, 4, 2)
-        collect(s_copy, 3, 7, 1, 6)
-        quantize_y(3, 6, 2)
-        store_codes(3, 6, 2)
-        for q in range(4):
+        planes(3, 4, 2)
+        collect(3, 7, 0, 1)
+        planes(3, 6, 2)
+        for q in range(QUADRANTS):
             (nc.sync, nc.scalar)[q % 2].dma_start(
                 out=out_2[:, 4 * q : 4 * q + 4, :].bitcast(I32),
                 in_=y_plane[32 * q : 32 * q + 16, :].bitcast(I32),

from contextlib import ExitStack

import concourse.mybir as mybir
from concourse.masks import make_identity

F32 = mybir.dt.float32
BF16 = mybir.dt.bfloat16
I32 = mybir.dt.int32
U32 = mybir.dt.uint32
U8 = mybir.dt.uint8
FP8X4 = mybir.dt.float8_e4m3fn_x4
ALU = mybir.AluOpType
ACT = mybir.ActivationFunctionType

P = 128
PACK = 4
K_PASS = P * PACK
MEMBERS = 8
QUAD = 4
CELLS = 2048
ROWS = MEMBERS * P
WIDTH = 512
CHUNKS = CELLS // WIDTH
PASSES = CELLS // K_PASS
PIECES = CHUNKS * PASSES
PAIRS = MEMBERS // 2
BANKS = 8
QUADRANTS = 4
FLOPS = 2 * ROWS * CELLS * CELLS

RAW_SLOTS = 10
MIXED_SLOTS = 4
ROUNDED_SLOTS = 8
TURNED_SLOTS = 4

CHUNK0_SHARE = 288
CHUNK1_SHARE = 256
CHUNK3_SHARE = 128


def tile_tracer_advect_decay_source_g6_kernel(
    tc, x_words, x_scales, advect, rate, source, out_0, out_1, out_2
):
    nc = tc.nc
    with ExitStack() as ctx:
        sb = ctx.enter_context(tc.tile_pool(name="sb", bufs=1))
        ps = ctx.enter_context(tc.psum_pool(name="ps", bufs=1))
        ctx.enter_context(tc.manual_schedule())

        def tiles(name, count, shape, dtype):
            return [sb.tile(shape, dtype, name="%s%d" % (name, i), align_bytes=64) for i in range(count)]

        banks = [ps.tile([P, WIDTH], F32, name="bank%d" % i) for i in range(BANKS)]
        x_low = tiles("x_low", PASSES, [P, QUAD * P], U32)
        x_high = tiles("x_high", 2, [P, PASSES, 2 * P], U32)
        x_plane = sb.tile([P, ROWS], U8, name="x_plane", align_bytes=64)
        a_raw = tiles("a_raw", RAW_SLOTS, [P, PACK, WIDTH], BF16)
        a_mixed = tiles("a_mixed", MIXED_SLOTS, [P, WIDTH, PACK], BF16)
        a_codes = tiles("a_codes", PIECES, [P, WIDTH], U32)
        a_plane = tiles("a_plane", PIECES, [P, WIDTH], U8)
        src = tiles("src", CHUNKS, [P, WIDTH], BF16)
        rate_col = sb.tile([P, 1], BF16, name="rate_col")
        decay = sb.tile([P, 1], F32, name="decay")
        ident = sb.tile([P, P], F32, name="ident")
        y = tiles("y", CHUNKS * PAIRS, [P, 2, WIDTH], F32)
        rounded = tiles("rounded", ROUNDED_SLOTS, [P, 2 * WIDTH], BF16)
        turned = tiles("turned", TURNED_SLOTS, [P, QUAD * P * PACK], BF16)
        y_codes = tiles("y_codes", CHUNKS, [P, ROWS], U32)
        y_plane = sb.tile([P, ROWS], U8, name="y_plane", align_bytes=64)

        vector_copy, scalar_copy = nc.vector.tensor_copy, nc.scalar.copy


        def load_a(piece):
            chunk, g = divmod(piece, PASSES)
            rows = advect[g * K_PASS : (g + 1) * K_PASS, chunk * WIDTH : (chunk + 1) * WIDTH]
            nc.sync.dma_start(out=a_raw[piece % RAW_SLOTS][:], in_=rows.rearrange("(p t) c -> p t c", t=PACK))

        def load_x_low(g):
            words = x_words[g].rearrange("p n t -> p (n t)").bitcast(I32)
            nc.sync.dma_start(out=x_low[g][:].bitcast(I32), in_=words[:, : QUAD * P])

        def load_x_high(half):
            words = x_words.rearrange("g p n t -> p g (n t)").bitcast(I32)
            cols = slice((QUAD + 2 * half) * P, (QUAD + 2 * half + 2) * P)
            nc.sync.dma_start(out=x_high[half][:].bitcast(I32), in_=words[:, :, cols])

        def load_src(chunk):
            nc.sync.dma_start(out=src[chunk][:], in_=source[:, chunk * WIDTH : (chunk + 1) * WIDTH])


        def interleave(chunk, g, vector_cols):
            piece = chunk * PASSES + g
            raw, mixed = a_raw[piece % RAW_SLOTS], a_mixed[piece % MIXED_SLOTS]
            for copy, lo, hi in ((vector_copy, 0, vector_cols), (scalar_copy, vector_cols, WIDTH)):
                if hi > lo:
                    copy(
                        out=mixed[:, lo:hi, :].rearrange("p (c i) t -> p c t i", i=4),
                        in_=raw[:, :, lo:hi].rearrange("p t (c i) -> p c t i", i=4),
                    )
            if piece + RAW_SLOTS < PIECES:
                load_a(piece + RAW_SLOTS)

        def quantize_a(chunk, g):
            piece = chunk * PASSES + g
            nc.vector.quantize_mx(
                out=a_codes[piece][:].bitcast(FP8X4),
                scales=a_plane[piece][:],
                in_=a_mixed[piece % MIXED_SLOTS][:].rearrange("p c t -> p (c t)"),
            )

        def x_operand(g, member):
            if member < QUAD:
                return x_low[g][:, member * P : (member + 1) * P]
            return x_high[(member - QUAD) // 2][:, g, (member % 2) * P : (member % 2 + 1) * P]

        def multiply(chunk, member, g):
            piece = chunk * PASSES + g
            nc.tensor.matmul_mx(
                out=banks[member][:],
                lhsT=x_operand(g, member).bitcast(FP8X4),
                lhsT_scale=x_plane[4 * g :, member * P : (member + 1) * P],
                rhs=a_codes[piece][:].bitcast(FP8X4),
                rhs_scale=a_plane[piece][:],
                start=(g == 0),
                stop=(g == PASSES - 1),
            )

        def sweep(chunk, g):
            for member in range(QUAD):
                multiply(chunk, member, g)

        def whole(chunk, member):
            for g in range(PASSES):
                multiply(chunk, member, g)


        def decay_and_source(out, flow, source_part):
            nc.vector.scalar_tensor_tensor(
                out=out, in0=flow, scalar=decay[:], in1=source_part, op0=ALU.mult, op1=ALU.add
            )

        def finish(chunk, member):
            decay_and_source(y[chunk * PAIRS + member // 2][:, member % 2, :], banks[member][:], src[chunk][:])

        def store_y(chunk, first, count):
            part = y[chunk * PAIRS + first // 2][:, first % 2 : first % 2 + count, :]
            rows = out_0[first : first + count, :, chunk * WIDTH : (chunk + 1) * WIDTH]
            nc.sync.dma_start(out=rows.rearrange("e r c -> r e c"), in_=part)

        def leave_pair(chunk, first):
            finish(chunk, first)
            finish(chunk, first + 1)
            store_y(chunk, first, 2)

        def leave_quad(chunk, first):
            leave_pair(chunk, first)
            leave_pair(chunk, first + 2)


        def rounded_tile(chunk, member):
            return rounded[(chunk * PAIRS + member // 2) % ROUNDED_SLOTS]

        def turned_tile(chunk, member):
            return turned[(2 * chunk + member // QUAD) % TURNED_SLOTS]

        def round_y(copy, chunk, first, count=2):
            lo, hi = first % 2, first % 2 + count
            copy(
                out=rounded_tile(chunk, first)[:, lo * WIDTH : hi * WIDTH].rearrange(
                    "r (m u p e) -> r m u p e", u=2, p=P, e=2
                ),
                in_=y[chunk * PAIRS + first // 2][:, lo:hi, :].rearrange("r m (p u e) -> r m u p e", u=2, e=2),
            )

        def round_quad(copy, chunk, first):
            round_y(copy, chunk, first)
            round_y(copy, chunk, first + 2)

        def finish_rounded(chunk, member):
            lo = (member % 2) * WIDTH
            words = rounded_tile(chunk, member)[:, lo : lo + WIDTH].rearrange("r (u p e) -> r u p e", u=2, e=2)
            flow = banks[member][:].rearrange("r (p u e) -> r u p e", u=2, e=2)
            source_part = src[chunk][:].rearrange("r (p u e) -> r u p e", u=2, e=2)
            for u in range(2):
                decay_and_source(words[:, u], flow[:, u], source_part[:, u])

        def turn(chunk, first, bank, count=2):
            words = rounded_tile(chunk, first)[:].bitcast(F32)
            for slot in range(2 * (first % 2), 2 * (first % 2 + count)):
                cols = slice(slot * P, (slot + 1) * P)
                nc.tensor.transpose(banks[bank][:, cols], words[:, cols], ident[:])

        def collect(chunk, first, bank, count=2):
            quad_words = turned_tile(chunk, first)[:].bitcast(F32)
            to, frm, size = 2 * P * (first % QUAD), 2 * P * (first % 2), 2 * P * count
            scalar_copy(
                out=quad_words[:, to : to + size].rearrange("p (m r u) -> p m r u", r=P, u=2),
                in_=banks[bank][:, frm : frm + size].rearrange("p (m u r) -> p m r u", u=2, r=P),
            )

        def turn_pairs(chunk, pairs, first_bank):
            for i, pair in enumerate(pairs):
                turn(chunk, 2 * pair, first_bank + i)

        def collect_pairs(chunk, pairs, first_bank):
            for i, pair in enumerate(pairs):
                collect(chunk, 2 * pair, first_bank + i)

        def planes(chunk, first, count=QUAD):
            cols = slice(first * P, (first + count) * P)
            lo = (first % QUAD) * K_PASS
            nc.vector.quantize_mx(
                out=y_codes[chunk][:, cols].bitcast(FP8X4),
                scales=y_plane[4 * chunk :, cols],
                in_=turned_tile(chunk, first)[:, lo : lo + count * K_PASS],
            )
            words = out_1[chunk].rearrange("p n t -> p (n t)").bitcast(I32)
            nc.sync.dma_start(out=words[:, cols], in_=y_codes[chunk][:, cols].bitcast(I32))

        all_pairs, low_pairs, high_pairs = range(PAIRS), range(2), range(2, PAIRS)

        nc.scalar.dma_start(out=rate_col[:], in_=rate.rearrange("(p o) -> p o", o=1))
        nc.vector.memset(x_plane[:].bitcast(I32), 0)
        load_a(0)
        for q in range(QUADRANTS):
            nc.sync.dma_start(
                out=x_plane[32 * q : 32 * q + 16, :].bitcast(I32),
                in_=x_scales[:, 4 * q : 4 * q + 4, :].bitcast(I32),
            )
        load_x_low(0)
        load_a(1)
        load_a(2)
        load_x_low(1)
        load_a(3)
        load_x_low(2)
        load_x_low(3)
        load_src(0)
        load_x_high(0)
        load_a(4)
        load_x_high(1)
        for piece in range(5, 8):
            load_a(piece)
        load_src(1)
        load_a(8)
        load_a(9)
        nc.scalar.activation(out=decay[:], in_=rate_col[:], func=ACT.Exp, scale=-1.0)
        make_identity(nc, ident[:])

        for g in range(PASSES):
            interleave(0, g, CHUNK0_SHARE)
            quantize_a(0, g)
            sweep(0, g)
            if g == 1:
                load_src(2)
        load_src(3)
        for member in range(QUAD, MEMBERS):
            whole(0, member)

        interleave(1, 0, 0)
        for member in range(QUAD):
            finish(0, member)
        round_y(vector_copy, 0, 0)
        for g in range(PASSES):
            if g < PASSES - 1:
                interleave(1, g + 1, CHUNK1_SHARE)
            quantize_a(1, g)
            sweep(1, g)
        store_y(0, 0, 2)
        store_y(0, 2, 2)
        interleave(2, 0, 0)
        leave_quad(0, QUAD)
        for member in range(QUAD, MEMBERS):
            whole(1, member)
        interleave(2, 1, 0)
        quantize_a(2, 0)
        leave_quad(1, 0)
        interleave(2, 2, 0)
        quantize_a(2, 1)
        round_y(vector_copy, 0, 2)
        round_y(vector_copy, 0, 4)
        interleave(2, 3, 0)
        quantize_a(2, 2)

        for g in range(PASSES - 1):
            sweep(2, g)
        leave_pair(1, 4)
        interleave(3, 0, 0)
        quantize_a(2, 3)
        sweep(2, 3)
        leave_pair(1, 6)
        round_y(vector_copy, 0, 6)
        turn_pairs(0, all_pairs, QUAD)
        round_y(scalar_copy, 1, 0)
        collect_pairs(0, all_pairs, QUAD)
        quantize_a(3, 0)
        leave_quad(2, 0)
        whole(2, 4)
        whole(2, 5)
        interleave(3, 1, CHUNK3_SHARE)
        round_y(vector_copy, 1, 2)
        round_quad(vector_copy, 1, QUAD)
        whole(2, 6)
        turn_pairs(1, all_pairs, 0)
        whole(2, 7)
        interleave(3, 2, CHUNK3_SHARE)
        quantize_a(3, 1)
        planes(0, 0)
        planes(0, QUAD)
        collect_pairs(1, all_pairs, 0)

        sweep(3, 0)
        sweep(3, 1)
        quantize_a(3, 2)
        interleave(3, 3, CHUNK3_SHARE)
        leave_quad(2, QUAD)
        sweep(3, 2)
        round_y(vector_copy, 2, 0)
        quantize_a(3, 3)
        sweep(3, 3)
        round_y(vector_copy, 2, 2)
        round_quad(scalar_copy, 2, QUAD)
        turn_pairs(2, all_pairs, QUAD)
        planes(1, 0)
        collect_pairs(2, low_pairs, QUAD)
        whole(3, 4)
        whole(3, 5)
        leave_quad(3, 0)
        round_y(scalar_copy, 3, 0)
        collect_pairs(2, high_pairs, QUAD + 2)
        planes(1, QUAD)
        round_y(vector_copy, 3, 2)
        turn_pairs(3, low_pairs, 0)
        whole(3, 6)
        whole(3, 7)
        planes(2, 0)
        finish(3, 4)
        planes(2, QUAD)
        finish(3, 5)
        store_y(3, 4, 2)
        collect_pairs(3, low_pairs, 0)
        round_y(scalar_copy, 3, 4)
        planes(3, 0)

        finish(3, 6)
        store_y(3, 6, 1)
        round_y(scalar_copy, 3, 6, 1)
        turn(3, 4, 2)
        turn(3, 6, 3, 1)
        finish_rounded(3, 7)
        collect(3, 4, 2)
        collect(3, 6, 3, 1)
        turn(3, 7, 0, 1)
        finish(3, 7)
        store_y(3, 7, 1)
        planes(3, 4, 2)
        collect(3, 7, 0, 1)
        planes(3, 6, 2)
        for q in range(QUADRANTS):
            (nc.sync, nc.scalar)[q % 2].dma_start(
                out=out_2[:, 4 * q : 4 * q + 4, :].bitcast(I32),
                in_=y_plane[32 * q : 32 * q + 16, :].bitcast(I32),
            )
